import numpy as np
import ml_dtypes


def mxq(x, axis, fmt="e4m3"):
    dtype, down = {"e4m3": (ml_dtypes.float8_e4m3fn, 7), "e5m2": (ml_dtypes.float8_e5m2, 14)}[fmt]
    v = np.moveaxis(np.asarray(x, np.float32).astype(ml_dtypes.bfloat16).astype(np.float64), axis, -1)
    blocks = v.reshape(v.shape[:-1] + (-1, 32))
    amax = np.abs(blocks).max(-1, keepdims=True)
    byte = np.maximum(np.where(amax > 0, np.frexp(amax)[1] - 1 + 127, 0) - down, 1)
    scale = np.exp2(byte - 127.0)
    codes = (blocks / scale).astype(np.float32).astype(dtype).astype(np.float64)
    return np.moveaxis((codes * scale).reshape(v.shape), -1, axis)


WIDE = False


def mx_kscale(k):
    if not WIDE:
        return np.ones(k)
    levels = np.array([10, -10, 5, -5, 0])
    if k % 512:
        return np.exp2(np.random.permutation(np.resize(levels, k // 32))).repeat(32)
    a = np.empty((k // 512, 16))
    for p in range(k // 512):
        a[p, :8] = np.random.permutation(np.resize(levels, 8))
        for g in range(8):
            far = levels[np.abs(levels - a[p, g]) >= 10]
            a[p, g + 8] = far[np.random.randint(len(far))]
    return np.exp2(a.ravel()).repeat(32)


def f64(x):
    return np.asarray(x).astype(np.float64)


def striped(idx):
    return np.tile(np.asarray(idx).reshape(-1, 16).T, (8, 1)).astype(np.uint16)


def unstriped(offs):
    return offs[:16].T.reshape(-1).astype(np.int64)


E2M1 = np.array([0.0, 0.5, 1.0, 1.5, 2.0, 3.0, 4.0, 6.0, -0.0, -0.5, -1.0, -1.5, -2.0, -3.0, -4.0, -6.0])


def pack_weight(w, fmt):
    k, n = w.shape
    w = f64(np.asarray(w, np.float32).astype(ml_dtypes.bfloat16)).reshape(k // 32, 32, n)
    amax = np.abs(w).max(1)
    if fmt == "e4m3":
        byte = np.frexp(amax)[1] - 1 + 127 - 7
    else:
        mant, ex = np.frexp(amax / 6.0)
        byte = np.where(mant > 0.5, ex, ex - 1) + 127
    byte = np.clip(np.where(amax > 0, byte, 1), 1, 254)
    scaled = (w * np.exp2(127.0 - byte)[:, None, :]).reshape(k, n).astype(np.float32)
    by_word = np.ascontiguousarray(scaled.reshape(k // 512, 128, 4, n).transpose(0, 1, 3, 2))
    if fmt == "e4m3":
        words = by_word.astype(ml_dtypes.float8_e4m3fn).view(np.uint8)
    else:
        c = by_word.astype(ml_dtypes.float4_e2m1fn).view(np.uint8) & 0xF
        words = (c[..., 0::2] | (c[..., 1::2] << 4)).reshape(k // 512, 128, 2 * n)
    return np.ascontiguousarray(words), np.ascontiguousarray(byte.astype(np.uint8).reshape(k // 512, 16, n))


def unpack_weight(words, scales, fmt):
    g, _, n = scales.shape
    words = np.ascontiguousarray(words).reshape(g, 128, n, -1)
    if fmt == "e4m3":
        vals = words.view(ml_dtypes.float8_e4m3fn).astype(np.float64)
    else:
        nib = np.empty((g, 128, n, 4), np.uint8)
        nib[..., 0::2] = words & 0xF
        nib[..., 1::2] = words >> 4
        vals = E2M1[nib]
    vals = vals * np.repeat(np.exp2(scales.astype(np.float64) - 127.0), 8, axis=1)[..., None]
    return vals.transpose(0, 1, 3, 2).reshape(g * 512, n)


def silu(v):
    return v / (1.0 + np.exp(-v))


D, K, R, T, I, Q, G = 512, 512, 512, 2048, 512, 128, 32


def setup_inputs():
    n = np.random.standard_normal
    idx = np.random.permutation(T)[:I]
    fd = mx_kscale(D)
    fk = mx_kscale(K)
    fr = mx_kscale(R)
    keysp = pack_weight(n((D, T)) / fd[:, None], "e4m3")
    tabp = pack_weight(n((K, T)) / fk[:, None], "e4m3")
    return {
        "query": (n((D, Q)) * 0.7 / np.sqrt(D) * fd[:, None]).astype(np.float32),
        "keys_words": keysp[0],
        "keys_scales": keysp[1],
        "tab_words": tabp[0],
        "tab_scales": tabp[1],
        "w1": (n((K, R)) * 1 / np.sqrt(K) * fk[:, None]).astype(np.float32),
        "gain": (np.random.uniform(0.7, 2.0, (R, 1))).astype(np.float32),
        "gout": (n((R, Q)) * 1 / np.sqrt(R) * fr[:, None]).astype(np.float32),
        "hsc": (np.random.uniform(0.7, 1.4, (R, 1)) / fr[:, None]).astype(np.float32),
        "old": (0.5 * n((Q, T))).astype(np.float32),
        "offs": striped(idx),
    }


def reference(query, keys_words, keys_scales, tab_words, tab_scales, w1, gain, gout, hsc, old, offs):
    idx = unstriped(offs)
    keysu = unpack_weight(keys_words, keys_scales, "e4m3")
    tabu = unpack_weight(tab_words, tab_scales, "e4m3")
    queryq = mxq(f64(query), 0, "e4m3")
    keysidxg = keysu[:, idx]
    a = queryq.T @ keysidxg
    p = np.exp(a - np.max(a, axis=1, keepdims=True))
    z = np.sum(p, axis=1, keepdims=True)
    w1q = mxq(f64(w1), 0, "e4m3")
    tabidxg = tabu[:, idx]
    zh = w1q.T @ tabidxg
    mz = np.sqrt(np.square(zh).reshape(R, G, I // G).mean(axis=2) + 0.1)
    mzr = np.repeat(mz, I // G, axis=1)
    hv = silu(zh / mzr * f64(gain))
    hs1 = hv * f64(hsc)
    goutq = mxq(f64(gout), 0, "e4m3")
    hs1q = mxq(hs1, 0, "e4m3")
    c0 = goutq.T @ hs1q
    dz = np.sum(c0 * p / np.square(z) * (-1.0), axis=1, keepdims=True)
    dp = c0 / z + dz
    da = dp * p
    gs = da * 512.0
    gf = np.zeros((Q, T))
    gf[:, idx] = gs
    y = f64(old) + gf
    return y

@@ -1,0 +1,210 @@
+from contextlib import ExitStack
+
+import concourse.mybir as mybir
+
+D, K, R, T, I, Q, G = 512, 512, 512, 2048, 512, 128, 32
+FLOPS = 2 * (D * Q * I + K * R * I + R * Q * I)
+
+F32 = mybir.dt.float32
+BF16 = mybir.dt.bfloat16
+I32 = mybir.dt.int32
+U32 = mybir.dt.uint32
+U16 = mybir.dt.uint16
+U8 = mybir.dt.uint8
+FP8X4 = mybir.dt.float8_e4m3fn_x4
+ALU = mybir.AluOpType
+ACT = mybir.ActivationFunctionType
+AXIS_X = mybir.AxisListType.X
+
+P = 128
+PACK = 4
+PAGE = I // G
+CHUNK = 128
+CHUNKS = I // CHUNK
+PAGES = CHUNK // PAGE
+OUT_CHUNK = 512
+
+
+def tile_attend_blrscaled_soft_kernel(
+    tc, query, keys_words, keys_scales, tab_words, tab_scales, w1, gain, gout, hsc, old, offs, out
+):
+    nc = tc.nc
+    with ExitStack() as ctx:
+        sb = ctx.enter_context(tc.tile_pool(name="sb", bufs=1))
+        ps = ctx.enter_context(tc.psum_pool(name="ps", bufs=1))
+
+        offsets = sb.tile([P, I // 16], U16, name="offsets")
+        nc.sync.dma_start(offsets[:], offs)
+
+        def load_scale_rows(queue, scales, name):
+            plane = sb.tile([P, T], U8, name=name, align_bytes=64)
+            nc.vector.memset(plane[:].bitcast(I32), 0)
+            for quad in range(4):
+                queue.dma_start(
+                    plane[32 * quad : 32 * quad + 4, :].bitcast(I32),
+                    scales[0, 4 * quad : 4 * quad + 4, :].bitcast(I32),
+                )
+            return plane
+
+        def load_words(words, name):
+            pool = sb.tile([P, T], I32, name=name, align_bytes=64)
+            nc.sync.dma_start(pool[:], words[0].rearrange("p n t -> p (n t)").bitcast(I32))
+            return pool
+
+        def load_rows(rows, name, tag):
+            raw = sb.tile([P, PACK, rows.shape[1]], F32, name=name, tag=tag, align_bytes=64)
+            nc.sync.dma_start(raw[:], rows.rearrange("(p j) c -> p j c", j=PACK))
+            return raw
+
+        w1_raw = load_rows(w1, "w1_raw", "wide_rows")
+        tab_scale_pool = load_scale_rows(nc.scalar, tab_scales, "tab_scale_pool")
+        tab_word_pool = load_words(tab_words, "tab_word_pool")
+        query_raw = load_rows(query, "query_raw", "narrow_rows")
+        key_word_pool = load_words(keys_words, "key_word_pool")
+        key_scale_pool = load_scale_rows(nc.gpsimd, keys_scales, "key_scale_pool")
+        gain_sb = sb.tile([P, PACK], F32, name="gain_sb")
+        nc.gpsimd.dma_start(gain_sb[:], gain.rearrange("(p t) o -> p (t o)", t=PACK))
+        hsc_sb = sb.tile([P, PACK], F32, name="hsc_sb")
+        nc.gpsimd.dma_start(hsc_sb[:], hsc.rearrange("(p t) o -> p (t o)", t=PACK))
+
+        placed = sb.tile([P, T], F32, name="placed")
+        nc.vector.memset(placed[:], 0.0)
+
+        def quantise(values, width, name):
+            codes = sb.tile([P, width], U32, name=name + "_codes", align_bytes=64)
+            scales = sb.tile([P, width], U8, name=name + "_scales", align_bytes=64)
+            nc.vector.quantize_mx(out=codes[:].bitcast(FP8X4), scales=scales[:], in_=values)
+            return codes, scales
+
+        def product(dst, stationary, stationary_cols, moving, moving_cols):
+            nc.tensor.matmul_mx(
+                out=dst,
+                lhsT=stationary[0][:, stationary_cols].bitcast(FP8X4),
+                lhsT_scale=stationary[1][:, stationary_cols],
+                rhs=moving[0][:, moving_cols].bitcast(FP8X4),
+                rhs_scale=moving[1][:, moving_cols],
+                start=True,
+                stop=True,
+            )
+
+        tab_scale = sb.tile([P, I], U8, name="tab_scale", align_bytes=64)
+        nc.vector.tensor_copy(tab_scale[:], tab_scale_pool[:].indirect(offsets[:]))
+
+        w1_bf = sb.tile([P, PACK, P, PACK], BF16, name="w1_bf", align_bytes=64)
+        w1_dst = w1_bf[:].rearrange("p t m j -> p m j t")
+        w1_src = w1_raw[:].rearrange("p j (m t) -> p m j t", t=PACK)
+        nc.vector.tensor_copy(w1_dst[:, : P // 2], w1_src[:, : P // 2])
+        nc.scalar.copy(w1_dst[:, P // 2 :], w1_src[:, P // 2 :])
+        w1_q = quantise(w1_bf[:].rearrange("p t m j -> p (t m j)"), R, "w1")
+
+        zh = []
+        mean_sq = sb.tile([P, CHUNKS, PAGES, PACK], F32, name="mean_sq")
+        for c in range(CHUNKS):
+            words = sb.tile([P, CHUNK], U32, name="tab_words%d" % c, align_bytes=64)
+            nc.vector.tensor_copy(
+                words[:], tab_word_pool[:].bitcast(U32).indirect(offsets[:, PAGES * c : PAGES * (c + 1)])
+            )
+            bank = ps.tile([P, PACK, CHUNK], F32, name="zh%d" % c)
+            for t in range(PACK):
+                nc.tensor.matmul_mx(
+                    out=bank[:, t, :],
+                    lhsT=w1_q[0][:, P * t : P * (t + 1)].bitcast(FP8X4),
+                    lhsT_scale=w1_q[1][:, P * t : P * (t + 1)],
+                    rhs=words[:].bitcast(FP8X4),
+                    rhs_scale=tab_scale[:, CHUNK * c : CHUNK * (c + 1)],
+                    start=True,
+                    stop=True,
+                )
+            zh.append(bank)
+
+        def interleave(raw, name):
+            bf = sb.tile([P, Q, PACK], BF16, name=name, align_bytes=64)
+            nc.scalar.copy(
+                bf[:].rearrange("p (c i) j -> p c j i", i=4), raw[:].rearrange("p j (c i) -> p c j i", i=4)
+            )
+            return bf[:].rearrange("p c j -> p (c j)")
+
+        old_sb = sb.tile([P, T], F32, name="old_sb", tag="wide_rows", align_bytes=64)
+        nc.sync.dma_start(old_sb[:], old)
+        query_bf = interleave(query_raw, "query_bf")
+        gout_raw = load_rows(gout, "gout_raw", "narrow_rows")
+
+        key_scale = sb.tile([P, I], U8, name="key_scale", tag="tab_word_pool", align_bytes=64)
+        nc.vector.tensor_copy(key_scale[:], key_scale_pool[:].indirect(offsets[:]))
+        query_q = quantise(query_bf, Q, "query")
+
+        for c in range(CHUNKS):
+            sq = sb.tile([P, PACK, CHUNK], F32, name="sq%d" % c)
+            nc.scalar.activation(sq[:], zh[c][:], ACT.Square)
+            nc.vector.tensor_reduce(
+                mean_sq[:, c], sq[:].rearrange("p t (g j) -> p g t j", j=PAGE), AXIS_X, ALU.add
+            )
+
+        inv_rms = sb.tile([P, CHUNKS * PAGES, PACK], F32, name="inv_rms")
+        nc.scalar.activation(
+            inv_rms[:], mean_sq[:].rearrange("p c g t -> p (c g) t"), ACT.Abs_reciprocal_sqrt, bias=0.1, scale=1.0 / PAGE
+        )
+
+        key_words = sb.tile([P, I], U32, name="key_words", align_bytes=64)
+        nc.vector.tensor_copy(key_words[:], key_word_pool[:].bitcast(U32).indirect(offsets[:]))
+        scores = ps.tile([P, I], F32, name="scores")
+        product(scores[:], query_q, slice(0, Q), (key_words, key_scale), slice(0, I))
+
+        factor = sb.tile([P, CHUNKS * PAGES, PACK], F32, name="factor")
+        nc.vector.tensor_tensor(
+            factor[:], inv_rms[:], gain_sb[:].unsqueeze(1).to_broadcast([P, CHUNKS * PAGES, PACK]), ALU.mult
+        )
+
+        activated = []
+        for c in range(CHUNKS):
+            pre = sb.tile([P, PAGES, PAGE, PACK], F32, name="pre%d" % c)
+            nc.vector.tensor_tensor(
+                pre[:],
+                zh[c][:].rearrange("p t (g j) -> p g j t", j=PAGE),
+                factor[:, PAGES * c : PAGES * (c + 1), :].unsqueeze(2).to_broadcast([P, PAGES, PAGE, PACK]),
+                ALU.mult,
+            )
+            hv = sb.tile([P, CHUNK, PACK], F32, name="hv%d" % c)
+            nc.scalar.activation(
+                hv[:].rearrange("p i t -> p (i t)"), pre[:].rearrange("p g j t -> p (g j t)"), ACT.Silu
+            )
+            activated.append(hv)
+
+        gout_bf = sb.tile([P, Q, PACK], BF16, name="gout_bf", align_bytes=64)
+        nc.gpsimd.tensor_copy(
+            gout_bf[:].rearrange("p (c i) j -> p c j i", i=4), gout_raw[:].rearrange("p j (c i) -> p c j i", i=4)
+        )
+        gout_q = quantise(gout_bf[:].rearrange("p c j -> p (c j)"), Q, "gout")
+
+        neg_max = sb.tile([P, 1], F32, name="neg_max")
+        nc.vector.tensor_reduce(neg_max[:], scores[:], AXIS_X, ALU.max, negate=True)
+
+        c0 = ps.tile([P, I], F32, name="c0")
+        for c in range(CHUNKS):
+            hs1 = sb.tile([P, CHUNK, PACK], BF16, name="hs1_%d" % c, align_bytes=64)
+            nc.vector.tensor_tensor(
+                hs1[:], activated[c][:], hsc_sb[:].unsqueeze(1).to_broadcast([P, CHUNK, PACK]), ALU.mult
+            )
+            hs1_q = quantise(hs1[:].rearrange("p i t -> p (i t)"), CHUNK, "hs1q%d" % c)
+            product(c0[:, CHUNK * c : CHUNK * (c + 1)], gout_q, slice(0, Q), hs1_q, slice(0, CHUNK))
+
+        p_exp = sb.tile([P, I], F32, name="p_exp")
+        z = sb.tile([P, 1], F32, name="z")
+        nc.scalar.activation(p_exp[:], scores[:], ACT.Exp, bias=neg_max[:], accum_out=z[:])
+        inv_z = sb.tile([P, 1], F32, name="inv_z")
+        nc.vector.reciprocal(inv_z[:], z[:])
+        weights = sb.tile([P, I], F32, name="weights")
+        nc.scalar.activation(weights[:], p_exp[:], ACT.Copy, scale=inv_z[:])
+
+        direct = sb.tile([P, I], F32, name="direct")
+        row_sum = sb.tile([P, 1], F32, name="row_sum")
+        nc.vector.scalar_tensor_tensor(direct[:], c0[:], 512.0, weights[:], ALU.mult, ALU.mult, accum_out=row_sum[:])
+        through_z = sb.tile([P, I], F32, name="through_z")
+        nc.vector.tensor_scalar(through_z[:], weights[:], row_sum[:], -1.0, ALU.mult, ALU.mult)
+        nc.vector.tensor_tensor(placed[:].indirect(offsets[:]), direct[:], through_z[:], ALU.add)
+
+        for c in range(T // OUT_CHUNK):
+            cols = slice(OUT_CHUNK * c, OUT_CHUNK * (c + 1))
+            result = sb.tile([P, OUT_CHUNK], F32, name="result%d" % c)
+            nc.vector.tensor_tensor(result[:], placed[:, cols], old_sb[:, cols], ALU.add)
+            (nc.sync if c % 2 == 0 else nc.scalar).dma_start(out[:, cols], result[:])

@@ -36,18 +36,18 @@ def tile_attend_blrscaled_soft_kernel(
         offsets = sb.tile([P, I // 16], U16, name="offsets")
         nc.sync.dma_start(offsets[:], offs)
 
-        def load_scale_rows(queue, scales, name):
-            plane = sb.tile([P, T], U8, name=name, align_bytes=64)
+        def load_scale_rows(scales, name, queues):
+            plane = sb.tile([P, T], U8, name=name, tag=name, align_bytes=64)
             nc.vector.memset(plane[:].bitcast(I32), 0)
             for quad in range(4):
-                queue.dma_start(
+                queues[quad].dma_start(
                     plane[32 * quad : 32 * quad + 4, :].bitcast(I32),
                     scales[0, 4 * quad : 4 * quad + 4, :].bitcast(I32),
                 )
             return plane
 
-        def load_words(words, name):
-            pool = sb.tile([P, T], I32, name=name, align_bytes=64)
+        def load_words(words, name, tag):
+            pool = sb.tile([P, T], I32, name=name, tag=tag, align_bytes=64)
             nc.sync.dma_start(pool[:], words[0].rearrange("p n t -> p (n t)").bitcast(I32))
             return pool
 
@@ -56,22 +56,27 @@ def tile_attend_blrscaled_soft_kernel(
             nc.sync.dma_start(raw[:], rows.rearrange("(p j) c -> p j c", j=PACK))
             return raw
 
-        w1_raw = load_rows(w1, "w1_raw", "wide_rows")
-        tab_scale_pool = load_scale_rows(nc.scalar, tab_scales, "tab_scale_pool")
-        tab_word_pool = load_words(tab_words, "tab_word_pool")
-        query_raw = load_rows(query, "query_raw", "narrow_rows")
-        key_word_pool = load_words(keys_words, "key_word_pool")
-        key_scale_pool = load_scale_rows(nc.gpsimd, keys_scales, "key_scale_pool")
-        gain_sb = sb.tile([P, PACK], F32, name="gain_sb")
-        nc.gpsimd.dma_start(gain_sb[:], gain.rearrange("(p t) o -> p (t o)", t=PACK))
+        def load_feature_vector(vector, repeats, name, tag):
+            raw = sb.tile([P, PACK], F32, name=name + "_raw", tag=tag, align_bytes=64)
+            nc.scalar.dma_start(raw[:], vector.rearrange("(p t) o -> p (t o)", t=PACK))
+            spread = sb.tile([P, repeats, PACK], F32, name=name + "_spread")
+            nc.vector.tensor_copy(spread[:], raw[:].unsqueeze(1).to_broadcast([P, repeats, PACK]))
+            return spread
+
+        w1_raw = load_rows(w1, "w1_raw", "first_wide")
+        tab_scale_pool = load_scale_rows(tab_scales, "tab_scale_pool", [nc.sync] * 4)
+        key_scale_pool = load_scale_rows(keys_scales, "key_scale_pool", [nc.sync] + [nc.gpsimd] * 3)
+        gain_sb = load_feature_vector(gain, G, "gain", "second_wide")
         hsc_sb = sb.tile([P, PACK], F32, name="hsc_sb")
         nc.gpsimd.dma_start(hsc_sb[:], hsc.rearrange("(p t) o -> p (t o)", t=PACK))
+        tab_word_pool = load_words(tab_words, "tab_word_pool", "second_wide")
 
-        placed = sb.tile([P, T], F32, name="placed")
-        nc.vector.memset(placed[:], 0.0)
+        constants = sb.tile([P, 2], F32, name="constants")
+        nc.vector.memset(constants[:, 0:1], 512.0)
+        nc.vector.memset(constants[:, 1:2], -1.0)
 
         def quantise(values, width, name):
-            codes = sb.tile([P, width], U32, name=name + "_codes", align_bytes=64)
+            codes = sb.tile([P, width], U32, name=name + "_codes", tag=name + "_codes", align_bytes=64)
             scales = sb.tile([P, width], U8, name=name + "_scales", align_bytes=64)
             nc.vector.quantize_mx(out=codes[:].bitcast(FP8X4), scales=scales[:], in_=values)
             return codes, scales
@@ -90,12 +95,19 @@ def tile_attend_blrscaled_soft_kernel(
         tab_scale = sb.tile([P, I], U8, name="tab_scale", align_bytes=64)
         nc.vector.tensor_copy(tab_scale[:], tab_scale_pool[:].indirect(offsets[:]))
 
-        w1_bf = sb.tile([P, PACK, P, PACK], BF16, name="w1_bf", align_bytes=64)
+        query_raw = load_rows(query, "query_raw", "tab_scale_pool")
+
+        w1_bf = sb.tile([P, PACK, P, PACK], BF16, name="w1_bf", tag="w1_bf", align_bytes=64)
         w1_dst = w1_bf[:].rearrange("p t m j -> p m j t")
         w1_src = w1_raw[:].rearrange("p j (m t) -> p m j t", t=PACK)
         nc.vector.tensor_copy(w1_dst[:, : P // 2], w1_src[:, : P // 2])
         nc.scalar.copy(w1_dst[:, P // 2 :], w1_src[:, P // 2 :])
+        key_scale = sb.tile([P, I], U8, name="key_scale", align_bytes=64)
+        nc.vector.tensor_copy(key_scale[:], key_scale_pool[:].indirect(offsets[:]))
         w1_q = quantise(w1_bf[:].rearrange("p t m j -> p (t m j)"), R, "w1")
+
+        key_word_pool = load_words(keys_words, "key_word_pool", "first_wide")
+        gout_raw = load_rows(gout, "gout_raw", "w1_bf")
 
         zh = []
         mean_sq = sb.tile([P, CHUNKS, PAGES, PACK], F32, name="mean_sq")
@@ -117,47 +129,48 @@ def tile_attend_blrscaled_soft_kernel(
                 )
             zh.append(bank)
 
-        def interleave(raw, name):
-            bf = sb.tile([P, Q, PACK], BF16, name=name, align_bytes=64)
+        def interleave(raw, name, tag):
+            bf = sb.tile([P, Q, PACK], BF16, name=name, tag=tag, align_bytes=64)
             nc.scalar.copy(
-                bf[:].rearrange("p (c i) j -> p c j i", i=4), raw[:].rearrange("p j (c i) -> p c j i", i=4)
+                bf[:].rearrange("p (c i) j -> p c j i", i=4), raw.rearrange("p j (c i) -> p c j i", i=4)
             )
             return bf[:].rearrange("p c j -> p (c j)")
 
-        old_sb = sb.tile([P, T], F32, name="old_sb", tag="wide_rows", align_bytes=64)
-        nc.sync.dma_start(old_sb[:], old)
-        query_bf = interleave(query_raw, "query_bf")
-        gout_raw = load_rows(gout, "gout_raw", "narrow_rows")
-
-        key_scale = sb.tile([P, I], U8, name="key_scale", tag="tab_word_pool", align_bytes=64)
-        nc.vector.tensor_copy(key_scale[:], key_scale_pool[:].indirect(offsets[:]))
+        query_bf = interleave(query_raw[:], "query_bf", "query_bf")
         query_q = quantise(query_bf, Q, "query")
 
         for c in range(CHUNKS):
-            sq = sb.tile([P, PACK, CHUNK], F32, name="sq%d" % c)
+            sq = sb.tile([P, PACK, CHUNK], F32, name="sq%d" % c, tag="sq%d" % c, align_bytes=64)
             nc.scalar.activation(sq[:], zh[c][:], ACT.Square)
             nc.vector.tensor_reduce(
                 mean_sq[:, c], sq[:].rearrange("p t (g j) -> p g t j", j=PAGE), AXIS_X, ALU.add
             )
+
+        gout_bf = interleave(gout_raw[:], "gout_bf", "w1_codes")
 
         inv_rms = sb.tile([P, CHUNKS * PAGES, PACK], F32, name="inv_rms")
         nc.scalar.activation(
             inv_rms[:], mean_sq[:].rearrange("p c g t -> p (c g) t"), ACT.Abs_reciprocal_sqrt, bias=0.1, scale=1.0 / PAGE
         )
 
-        key_words = sb.tile([P, I], U32, name="key_words", align_bytes=64)
+        key_words = sb.tile([P, I], U32, name="key_words", tag="sq%d" % (CHUNKS - 1), align_bytes=64)
         nc.vector.tensor_copy(key_words[:], key_word_pool[:].bitcast(U32).indirect(offsets[:]))
+        placed = sb.tile([P, T], F32, name="placed", tag="first_wide", align_bytes=64)
+        nc.gpsimd.memset(placed[:], 0.0)
         scores = ps.tile([P, I], F32, name="scores")
         product(scores[:], query_q, slice(0, Q), (key_words, key_scale), slice(0, I))
+        old_sb = sb.tile([P, T], F32, name="old_sb", tag="second_wide", align_bytes=64)
+        nc.sync.dma_start(old_sb[:], old)
 
+        gout_q = quantise(gout_bf, Q, "gout")
         factor = sb.tile([P, CHUNKS * PAGES, PACK], F32, name="factor")
         nc.vector.tensor_tensor(
-            factor[:], inv_rms[:], gain_sb[:].unsqueeze(1).to_broadcast([P, CHUNKS * PAGES, PACK]), ALU.mult
+            factor[:], inv_rms[:], gain_sb[:], ALU.mult
         )
 
         activated = []
         for c in range(CHUNKS):
-            pre = sb.tile([P, PAGES, PAGE, PACK], F32, name="pre%d" % c)
+            pre = sb.tile([P, PAGES, PAGE, PACK], F32, name="pre%d" % c, tag="pre%d" % c)
             nc.vector.tensor_tensor(
                 pre[:],
                 zh[c][:].rearrange("p t (g j) -> p g j t", j=PAGE),
@@ -170,37 +183,36 @@ def tile_attend_blrscaled_soft_kernel(
             )
             activated.append(hv)
 
-        gout_bf = sb.tile([P, Q, PACK], BF16, name="gout_bf", align_bytes=64)
-        nc.gpsimd.tensor_copy(
-            gout_bf[:].rearrange("p (c i) j -> p c j i", i=4), gout_raw[:].rearrange("p j (c i) -> p c j i", i=4)
-        )
-        gout_q = quantise(gout_bf[:].rearrange("p c j -> p (c j)"), Q, "gout")
-
         neg_max = sb.tile([P, 1], F32, name="neg_max")
         nc.vector.tensor_reduce(neg_max[:], scores[:], AXIS_X, ALU.max, negate=True)
 
         c0 = ps.tile([P, I], F32, name="c0")
-        for c in range(CHUNKS):
-            hs1 = sb.tile([P, CHUNK, PACK], BF16, name="hs1_%d" % c, align_bytes=64)
-            nc.vector.tensor_tensor(
-                hs1[:], activated[c][:], hsc_sb[:].unsqueeze(1).to_broadcast([P, CHUNK, PACK]), ALU.mult
-            )
-            hs1_q = quantise(hs1[:].rearrange("p i t -> p (i t)"), CHUNK, "hs1q%d" % c)
-            product(c0[:, CHUNK * c : CHUNK * (c + 1)], gout_q, slice(0, Q), hs1_q, slice(0, CHUNK))
+        hs1 = []
+        for step in range(CHUNKS + 1):
+            if step < CHUNKS:
+                scaled = sb.tile([P, CHUNK, PACK], BF16, name="hs1_%d" % step, align_bytes=64)
+                nc.vector.tensor_tensor(scaled[:], activated[step][:], hsc_sb[:].unsqueeze(1).to_broadcast([P, CHUNK, PACK]), ALU.mult)
+                hs1.append(scaled)
+            if step > 0:
+                c = step - 1
+                hs1_q = quantise(hs1[c][:].rearrange("p i t -> p (i t)"), CHUNK, "hs1q%d" % c)
+                product(c0[:, CHUNK * c : CHUNK * (c + 1)], gout_q, slice(0, Q), hs1_q, slice(0, CHUNK))
 
-        p_exp = sb.tile([P, I], F32, name="p_exp")
+        p_exp = sb.tile([P, I], F32, name="p_exp", tag="pre%d" % (CHUNKS - 1))
         z = sb.tile([P, 1], F32, name="z")
         nc.scalar.activation(p_exp[:], scores[:], ACT.Exp, bias=neg_max[:], accum_out=z[:])
         inv_z = sb.tile([P, 1], F32, name="inv_z")
         nc.vector.reciprocal(inv_z[:], z[:])
-        weights = sb.tile([P, I], F32, name="weights")
-        nc.scalar.activation(weights[:], p_exp[:], ACT.Copy, scale=inv_z[:])
+        row_factors = sb.tile([P, 2], F32, name="row_factors")
+        nc.vector.tensor_scalar(row_factors[:], constants[:], inv_z[:], None, ALU.mult)
 
         direct = sb.tile([P, I], F32, name="direct")
         row_sum = sb.tile([P, 1], F32, name="row_sum")
-        nc.vector.scalar_tensor_tensor(direct[:], c0[:], 512.0, weights[:], ALU.mult, ALU.mult, accum_out=row_sum[:])
+        nc.vector.scalar_tensor_tensor(
+            direct[:], c0[:], row_factors[:, 0:1], p_exp[:], ALU.mult, ALU.mult, accum_out=row_sum[:]
+        )
         through_z = sb.tile([P, I], F32, name="through_z")
-        nc.vector.tensor_scalar(through_z[:], weights[:], row_sum[:], -1.0, ALU.mult, ALU.mult)
+        nc.vector.tensor_scalar(through_z[:], p_exp[:], row_sum[:], row_factors[:, 1:2], ALU.mult, ALU.mult)
         nc.vector.tensor_tensor(placed[:].indirect(offsets[:]), direct[:], through_z[:], ALU.add)
 
         for c in range(T // OUT_CHUNK):

@@ -36,11 +36,11 @@ def tile_attend_blrscaled_soft_kernel(
         offsets = sb.tile([P, I // 16], U16, name="offsets")
         nc.sync.dma_start(offsets[:], offs)
 
-        def load_scale_rows(scales, name, queues):
-            plane = sb.tile([P, T], U8, name=name, tag=name, align_bytes=64)
+        def load_scale_rows(scales, name):
+            plane = sb.tile([P, T], U8, name=name, tag="scale_pool", align_bytes=64)
             nc.vector.memset(plane[:].bitcast(I32), 0)
             for quad in range(4):
-                queues[quad].dma_start(
+                nc.sync.dma_start(
                     plane[32 * quad : 32 * quad + 4, :].bitcast(I32),
                     scales[0, 4 * quad : 4 * quad + 4, :].bitcast(I32),
                 )
@@ -64,12 +64,14 @@ def tile_attend_blrscaled_soft_kernel(
             return spread
 
         w1_raw = load_rows(w1, "w1_raw", "first_wide")
-        tab_scale_pool = load_scale_rows(tab_scales, "tab_scale_pool", [nc.sync] * 4)
-        key_scale_pool = load_scale_rows(keys_scales, "key_scale_pool", [nc.sync] + [nc.gpsimd] * 3)
+        tab_scale_pool = load_scale_rows(tab_scales, "tab_scale_pool")
         gain_sb = load_feature_vector(gain, G, "gain", "second_wide")
-        hsc_sb = sb.tile([P, PACK], F32, name="hsc_sb")
-        nc.gpsimd.dma_start(hsc_sb[:], hsc.rearrange("(p t) o -> p (t o)", t=PACK))
+        hsc_sb = load_feature_vector(hsc, CHUNK, "hsc", "narrow")
         tab_word_pool = load_words(tab_words, "tab_word_pool", "second_wide")
+        query_raw = load_rows(query, "query_raw", "narrow")
+
+        placed = sb.tile([P, T], F32, name="placed")
+        nc.vector.memset(placed[:], 0.0)
 
         constants = sb.tile([P, 2], F32, name="constants")
         nc.vector.memset(constants[:, 0:1], 512.0)
@@ -95,15 +97,13 @@ def tile_attend_blrscaled_soft_kernel(
         tab_scale = sb.tile([P, I], U8, name="tab_scale", align_bytes=64)
         nc.vector.tensor_copy(tab_scale[:], tab_scale_pool[:].indirect(offsets[:]))
 
-        query_raw = load_rows(query, "query_raw", "tab_scale_pool")
+        key_scale_pool = load_scale_rows(keys_scales, "key_scale_pool")
 
         w1_bf = sb.tile([P, PACK, P, PACK], BF16, name="w1_bf", tag="w1_bf", align_bytes=64)
         w1_dst = w1_bf[:].rearrange("p t m j -> p m j t")
         w1_src = w1_raw[:].rearrange("p j (m t) -> p m j t", t=PACK)
         nc.vector.tensor_copy(w1_dst[:, : P // 2], w1_src[:, : P // 2])
         nc.scalar.copy(w1_dst[:, P // 2 :], w1_src[:, P // 2 :])
-        key_scale = sb.tile([P, I], U8, name="key_scale", align_bytes=64)
-        nc.vector.tensor_copy(key_scale[:], key_scale_pool[:].indirect(offsets[:]))
         w1_q = quantise(w1_bf[:].rearrange("p t m j -> p (t m j)"), R, "w1")
 
         key_word_pool = load_words(keys_words, "key_word_pool", "first_wide")
@@ -137,6 +137,8 @@ def tile_attend_blrscaled_soft_kernel(
             return bf[:].rearrange("p c j -> p (c j)")
 
         query_bf = interleave(query_raw[:], "query_bf", "query_bf")
+        key_scale = sb.tile([P, I], U8, name="key_scale", tag="second_wide", align_bytes=64)
+        nc.vector.tensor_copy(key_scale[:], key_scale_pool[:].indirect(offsets[:]))
         query_q = quantise(query_bf, Q, "query")
 
         for c in range(CHUNKS):
@@ -155,18 +157,17 @@ def tile_attend_blrscaled_soft_kernel(
 
         key_words = sb.tile([P, I], U32, name="key_words", tag="sq%d" % (CHUNKS - 1), align_bytes=64)
         nc.vector.tensor_copy(key_words[:], key_word_pool[:].bitcast(U32).indirect(offsets[:]))
-        placed = sb.tile([P, T], F32, name="placed", tag="first_wide", align_bytes=64)
-        nc.gpsimd.memset(placed[:], 0.0)
         scores = ps.tile([P, I], F32, name="scores")
         product(scores[:], query_q, slice(0, Q), (key_words, key_scale), slice(0, I))
         old_sb = sb.tile([P, T], F32, name="old_sb", tag="second_wide", align_bytes=64)
         nc.sync.dma_start(old_sb[:], old)
 
-        gout_q = quantise(gout_bf, Q, "gout")
         factor = sb.tile([P, CHUNKS * PAGES, PACK], F32, name="factor")
         nc.vector.tensor_tensor(
             factor[:], inv_rms[:], gain_sb[:], ALU.mult
         )
+
+        gout_q = quantise(gout_bf, Q, "gout")
 
         activated = []
         for c in range(CHUNKS):
@@ -191,7 +192,7 @@ def tile_attend_blrscaled_soft_kernel(
         for step in range(CHUNKS + 1):
             if step < CHUNKS:
                 scaled = sb.tile([P, CHUNK, PACK], BF16, name="hs1_%d" % step, align_bytes=64)
-                nc.vector.tensor_tensor(scaled[:], activated[step][:], hsc_sb[:].unsqueeze(1).to_broadcast([P, CHUNK, PACK]), ALU.mult)
+                nc.vector.tensor_tensor(scaled[:], activated[step][:], hsc_sb[:], ALU.mult)
                 hs1.append(scaled)
             if step > 0:
                 c = step - 1

@@ -22,7 +22,8 @@ PAGE = I // G
 CHUNK = 128
 CHUNKS = I // CHUNK
 PAGES = CHUNK // PAGE
-OUT_CHUNK = 512
+W1_SPLIT = 48
+OUT_WIDTHS = (512, 512, 512, 256, 256)
 
 
 def tile_attend_blrscaled_soft_kernel(
@@ -36,11 +37,11 @@ def tile_attend_blrscaled_soft_kernel(
         offsets = sb.tile([P, I // 16], U16, name="offsets")
         nc.sync.dma_start(offsets[:], offs)
 
-        def load_scale_rows(scales, name):
-            plane = sb.tile([P, T], U8, name=name, tag="scale_pool", align_bytes=64)
+        def load_scale_rows(queue, scales, name):
+            plane = sb.tile([P, T], U8, name=name, align_bytes=64)
             nc.vector.memset(plane[:].bitcast(I32), 0)
             for quad in range(4):
-                nc.sync.dma_start(
+                queue.dma_start(
                     plane[32 * quad : 32 * quad + 4, :].bitcast(I32),
                     scales[0, 4 * quad : 4 * quad + 4, :].bitcast(I32),
                 )
@@ -56,25 +57,21 @@ def tile_attend_blrscaled_soft_kernel(
             nc.sync.dma_start(raw[:], rows.rearrange("(p j) c -> p j c", j=PACK))
             return raw
 
-        def load_feature_vector(vector, repeats, name, tag):
-            raw = sb.tile([P, PACK], F32, name=name + "_raw", tag=tag, align_bytes=64)
-            nc.scalar.dma_start(raw[:], vector.rearrange("(p t) o -> p (t o)", t=PACK))
-            spread = sb.tile([P, repeats, PACK], F32, name=name + "_spread")
-            nc.vector.tensor_copy(spread[:], raw[:].unsqueeze(1).to_broadcast([P, repeats, PACK]))
-            return spread
+        def load_feature_vector(vector, name, tag):
+            values = sb.tile([P, PACK], F32, name=name, tag=tag, align_bytes=64)
+            nc.sync.dma_start(values[:], vector.rearrange("(p t) o -> p (t o)", t=PACK))
+            return values
 
-        w1_raw = load_rows(w1, "w1_raw", "first_wide")
-        tab_scale_pool = load_scale_rows(tab_scales, "tab_scale_pool")
-        gain_sb = load_feature_vector(gain, G, "gain", "second_wide")
-        hsc_sb = load_feature_vector(hsc, CHUNK, "hsc", "narrow")
-        tab_word_pool = load_words(tab_words, "tab_word_pool", "second_wide")
-        query_raw = load_rows(query, "query_raw", "narrow")
-
+        w1_raw = load_rows(w1, "w1_raw", "w1_raw")
+        tab_scale_pool = load_scale_rows(nc.sync, tab_scales, "tab_scale_pool")
+        tab_word_pool = load_words(tab_words, "tab_word_pool", "tab_word_pool")
+        query_raw = load_rows(query, "query_raw", "query_raw")
         placed = sb.tile([P, T], F32, name="placed")
         nc.vector.memset(placed[:], 0.0)
+        key_scale_pool = load_scale_rows(nc.sync, keys_scales, "key_scale_pool")
 
         constants = sb.tile([P, 2], F32, name="constants")
-        nc.vector.memset(constants[:, 0:1], 512.0)
+        nc.vector.memset(constants[:, 0:1], 1.0 / 512.0)
         nc.vector.memset(constants[:, 1:2], -1.0)
 
         def quantise(values, width, name):
@@ -94,35 +91,35 @@ def tile_attend_blrscaled_soft_kernel(
                 stop=True,
             )
 
-        tab_scale = sb.tile([P, I], U8, name="tab_scale", align_bytes=64)
-        nc.vector.tensor_copy(tab_scale[:], tab_scale_pool[:].indirect(offsets[:]))
-
-        key_scale_pool = load_scale_rows(keys_scales, "key_scale_pool")
-
         w1_bf = sb.tile([P, PACK, P, PACK], BF16, name="w1_bf", tag="w1_bf", align_bytes=64)
         w1_dst = w1_bf[:].rearrange("p t m j -> p m j t")
         w1_src = w1_raw[:].rearrange("p j (m t) -> p m j t", t=PACK)
-        nc.vector.tensor_copy(w1_dst[:, : P // 2], w1_src[:, : P // 2])
-        nc.scalar.copy(w1_dst[:, P // 2 :], w1_src[:, P // 2 :])
+        nc.vector.tensor_copy(w1_dst[:, :W1_SPLIT], w1_src[:, :W1_SPLIT])
+        nc.scalar.copy(w1_dst[:, W1_SPLIT:], w1_src[:, W1_SPLIT:])
+        tab_scale = sb.tile([P, I], U8, name="tab_scale", align_bytes=64)
+        nc.vector.tensor_copy(tab_scale[:], tab_scale_pool[:].indirect(offsets[:]))
         w1_q = quantise(w1_bf[:].rearrange("p t m j -> p (t m j)"), R, "w1")
 
-        key_word_pool = load_words(keys_words, "key_word_pool", "first_wide")
-        gout_raw = load_rows(gout, "gout_raw", "w1_bf")
+        gout_raw = load_rows(gout, "gout_raw", "w1_raw")
+        key_word_pool = load_words(keys_words, "key_word_pool", "w1_bf")
 
         zh = []
         mean_sq = sb.tile([P, CHUNKS, PAGES, PACK], F32, name="mean_sq")
-        for c in range(CHUNKS):
-            words = sb.tile([P, CHUNK], U32, name="tab_words%d" % c, align_bytes=64)
+        tab_pieces = []
+        for first, count in ((0, 1), (1, 1), (2, 2)):
+            words = sb.tile([P, count * CHUNK], U32, name="tab_words%d" % first, align_bytes=64)
             nc.vector.tensor_copy(
-                words[:], tab_word_pool[:].bitcast(U32).indirect(offsets[:, PAGES * c : PAGES * (c + 1)])
+                words[:], tab_word_pool[:].bitcast(U32).indirect(offsets[:, PAGES * first : PAGES * (first + count)])
             )
+            tab_pieces.extend(words[:, CHUNK * n : CHUNK * (n + 1)] for n in range(count))
+        for c in range(CHUNKS):
             bank = ps.tile([P, PACK, CHUNK], F32, name="zh%d" % c)
             for t in range(PACK):
                 nc.tensor.matmul_mx(
                     out=bank[:, t, :],
                     lhsT=w1_q[0][:, P * t : P * (t + 1)].bitcast(FP8X4),
                     lhsT_scale=w1_q[1][:, P * t : P * (t + 1)],
-                    rhs=words[:].bitcast(FP8X4),
+                    rhs=tab_pieces[c].bitcast(FP8X4),
                     rhs_scale=tab_scale[:, CHUNK * c : CHUNK * (c + 1)],
                     start=True,
                     stop=True,
@@ -137,9 +134,11 @@ def tile_attend_blrscaled_soft_kernel(
             return bf[:].rearrange("p c j -> p (c j)")
 
         query_bf = interleave(query_raw[:], "query_bf", "query_bf")
-        key_scale = sb.tile([P, I], U8, name="key_scale", tag="second_wide", align_bytes=64)
+        gain_sb = load_feature_vector(gain, "gain_sb", "query_raw")
+        key_scale = sb.tile([P, I], U8, name="key_scale", tag="tab_word_pool", align_bytes=64)
         nc.vector.tensor_copy(key_scale[:], key_scale_pool[:].indirect(offsets[:]))
         query_q = quantise(query_bf, Q, "query")
+        hsc_sb = load_feature_vector(hsc, "hsc_sb", "query_bf")
 
         for c in range(CHUNKS):
             sq = sb.tile([P, PACK, CHUNK], F32, name="sq%d" % c, tag="sq%d" % c, align_bytes=64)
@@ -159,12 +158,12 @@ def tile_attend_blrscaled_soft_kernel(
         nc.vector.tensor_copy(key_words[:], key_word_pool[:].bitcast(U32).indirect(offsets[:]))
         scores = ps.tile([P, I], F32, name="scores")
         product(scores[:], query_q, slice(0, Q), (key_words, key_scale), slice(0, I))
-        old_sb = sb.tile([P, T], F32, name="old_sb", tag="second_wide", align_bytes=64)
+        old_sb = sb.tile([P, T], F32, name="old_sb", tag="tab_word_pool", align_bytes=64)
         nc.sync.dma_start(old_sb[:], old)
 
         factor = sb.tile([P, CHUNKS * PAGES, PACK], F32, name="factor")
-        nc.vector.tensor_tensor(
-            factor[:], inv_rms[:], gain_sb[:], ALU.mult
+        nc.gpsimd.tensor_tensor(
+            factor[:], inv_rms[:], gain_sb[:].unsqueeze(1).to_broadcast([P, G, PACK]), ALU.mult
         )
 
         gout_q = quantise(gout_bf, Q, "gout")
@@ -188,24 +187,36 @@ def tile_attend_blrscaled_soft_kernel(
         nc.vector.tensor_reduce(neg_max[:], scores[:], AXIS_X, ALU.max, negate=True)
 
         c0 = ps.tile([P, I], F32, name="c0")
-        hs1 = []
-        for step in range(CHUNKS + 1):
-            if step < CHUNKS:
-                scaled = sb.tile([P, CHUNK, PACK], BF16, name="hs1_%d" % step, align_bytes=64)
-                nc.vector.tensor_tensor(scaled[:], activated[step][:], hsc_sb[:], ALU.mult)
-                hs1.append(scaled)
-            if step > 0:
-                c = step - 1
-                hs1_q = quantise(hs1[c][:].rearrange("p i t -> p (i t)"), CHUNK, "hs1q%d" % c)
-                product(c0[:, CHUNK * c : CHUNK * (c + 1)], gout_q, slice(0, Q), hs1_q, slice(0, CHUNK))
+        hs1 = sb.tile([P, I, PACK], BF16, name="hs1", align_bytes=64)
+
+        def scale_chunk(engine, c):
+            engine.tensor_tensor(
+                hs1[:, CHUNK * c : CHUNK * (c + 1), :],
+                activated[c][:],
+                hsc_sb[:].unsqueeze(1).to_broadcast([P, CHUNK, PACK]),
+                ALU.mult,
+            )
+
+        def read_gradient(first, count):
+            slots = slice(CHUNK * first, CHUNK * (first + count))
+            hs1_q = quantise(hs1[:, slots, :].rearrange("p i t -> p (i t)"), count * CHUNK, "hs1q%d" % first)
+            product(c0[:, slots], gout_q, slice(0, Q), hs1_q, slice(0, count * CHUNK))
+
+        scale_chunk(nc.gpsimd, 0)
+        scale_chunk(nc.vector, 1)
+        scale_chunk(nc.vector, 2)
+        read_gradient(0, 2)
+        scale_chunk(nc.vector, 3)
+        read_gradient(2, 1)
+        read_gradient(3, 1)
 
         p_exp = sb.tile([P, I], F32, name="p_exp", tag="pre%d" % (CHUNKS - 1))
         z = sb.tile([P, 1], F32, name="z")
         nc.scalar.activation(p_exp[:], scores[:], ACT.Exp, bias=neg_max[:], accum_out=z[:])
-        inv_z = sb.tile([P, 1], F32, name="inv_z")
-        nc.vector.reciprocal(inv_z[:], z[:])
+        scaled_z = sb.tile([P, 2], F32, name="scaled_z")
+        nc.scalar.activation(scaled_z[:], constants[:], ACT.Copy, scale=z[:])
         row_factors = sb.tile([P, 2], F32, name="row_factors")
-        nc.vector.tensor_scalar(row_factors[:], constants[:], inv_z[:], None, ALU.mult)
+        nc.vector.reciprocal(row_factors[:], scaled_z[:])
 
         direct = sb.tile([P, I], F32, name="direct")
         row_sum = sb.tile([P, 1], F32, name="row_sum")
@@ -216,8 +227,10 @@ def tile_attend_blrscaled_soft_kernel(
         nc.vector.tensor_scalar(through_z[:], p_exp[:], row_sum[:], row_factors[:, 1:2], ALU.mult, ALU.mult)
         nc.vector.tensor_tensor(placed[:].indirect(offsets[:]), direct[:], through_z[:], ALU.add)
 
-        for c in range(T // OUT_CHUNK):
-            cols = slice(OUT_CHUNK * c, OUT_CHUNK * (c + 1))
-            result = sb.tile([P, OUT_CHUNK], F32, name="result%d" % c)
+        start = 0
+        for c, width in enumerate(OUT_WIDTHS):
+            cols = slice(start, start + width)
+            result = sb.tile([P, width], F32, name="result%d" % c)
             nc.vector.tensor_tensor(result[:], placed[:, cols], old_sb[:, cols], ALU.add)
             (nc.sync if c % 2 == 0 else nc.scalar).dma_start(out[:, cols], result[:])
+            start = start + width

from contextlib import ExitStack

import concourse.mybir as mybir

D, K, R, T, I, Q, G = 512, 512, 512, 2048, 512, 128, 32
FLOPS = 2 * (D * Q * I + K * R * I + R * Q * I)

F32 = mybir.dt.float32
BF16 = mybir.dt.bfloat16
I32 = mybir.dt.int32
U32 = mybir.dt.uint32
U16 = mybir.dt.uint16
U8 = mybir.dt.uint8
FP8X4 = mybir.dt.float8_e4m3fn_x4
ALU = mybir.AluOpType
ACT = mybir.ActivationFunctionType
AXIS_X = mybir.AxisListType.X

P = 128
PACK = 4
PAGE = I // G
CHUNK = 128
CHUNKS = I // CHUNK
PAGES = CHUNK // PAGE
W1_SPLIT = 48
OUT_WIDTHS = (512, 512, 512, 256, 256)


def tile_attend_blrscaled_soft_kernel(
    tc, query, keys_words, keys_scales, tab_words, tab_scales, w1, gain, gout, hsc, old, offs, out
):
    nc = tc.nc
    with ExitStack() as ctx:
        sb = ctx.enter_context(tc.tile_pool(name="sb", bufs=1))
        ps = ctx.enter_context(tc.psum_pool(name="ps", bufs=1))

        offsets = sb.tile([P, I // 16], U16, name="offsets")
        nc.sync.dma_start(offsets[:], offs)

        def load_scale_rows(queue, scales, name):
            plane = sb.tile([P, T], U8, name=name, align_bytes=64)
            nc.vector.memset(plane[:].bitcast(I32), 0)
            for quad in range(4):
                queue.dma_start(
                    plane[32 * quad : 32 * quad + 4, :].bitcast(I32),
                    scales[0, 4 * quad : 4 * quad + 4, :].bitcast(I32),
                )
            return plane

        def load_words(words, name, tag):
            pool = sb.tile([P, T], I32, name=name, tag=tag, align_bytes=64)
            nc.sync.dma_start(pool[:], words[0].rearrange("p n t -> p (n t)").bitcast(I32))
            return pool

        def load_rows(rows, name, tag):
            raw = sb.tile([P, PACK, rows.shape[1]], F32, name=name, tag=tag, align_bytes=64)
            nc.sync.dma_start(raw[:], rows.rearrange("(p j) c -> p j c", j=PACK))
            return raw

        def load_feature_vector(vector, name, tag):
            values = sb.tile([P, PACK], F32, name=name, tag=tag, align_bytes=64)
            nc.sync.dma_start(values[:], vector.rearrange("(p t) o -> p (t o)", t=PACK))
            return values

        w1_raw = load_rows(w1, "w1_raw", "w1_raw")
        tab_scale_pool = load_scale_rows(nc.sync, tab_scales, "tab_scale_pool")
        tab_word_pool = load_words(tab_words, "tab_word_pool", "tab_word_pool")
        query_raw = load_rows(query, "query_raw", "query_raw")
        placed = sb.tile([P, T], F32, name="placed")
        nc.vector.memset(placed[:], 0.0)
        key_scale_pool = load_scale_rows(nc.sync, keys_scales, "key_scale_pool")

        constants = sb.tile([P, 2], F32, name="constants")
        nc.vector.memset(constants[:, 0:1], 1.0 / 512.0)
        nc.vector.memset(constants[:, 1:2], -1.0)

        def quantise(values, width, name):
            codes = sb.tile([P, width], U32, name=name + "_codes", tag=name + "_codes", align_bytes=64)
            scales = sb.tile([P, width], U8, name=name + "_scales", align_bytes=64)
            nc.vector.quantize_mx(out=codes[:].bitcast(FP8X4), scales=scales[:], in_=values)
            return codes, scales

        def product(dst, stationary, stationary_cols, moving, moving_cols):
            nc.tensor.matmul_mx(
                out=dst,
                lhsT=stationary[0][:, stationary_cols].bitcast(FP8X4),
                lhsT_scale=stationary[1][:, stationary_cols],
                rhs=moving[0][:, moving_cols].bitcast(FP8X4),
                rhs_scale=moving[1][:, moving_cols],
                start=True,
                stop=True,
            )

        w1_bf = sb.tile([P, PACK, P, PACK], BF16, name="w1_bf", tag="w1_bf", align_bytes=64)
        w1_dst = w1_bf[:].rearrange("p t m j -> p m j t")
        w1_src = w1_raw[:].rearrange("p j (m t) -> p m j t", t=PACK)
        nc.vector.tensor_copy(w1_dst[:, :W1_SPLIT], w1_src[:, :W1_SPLIT])
        nc.scalar.copy(w1_dst[:, W1_SPLIT:], w1_src[:, W1_SPLIT:])
        tab_scale = sb.tile([P, I], U8, name="tab_scale", align_bytes=64)
        nc.vector.tensor_copy(tab_scale[:], tab_scale_pool[:].indirect(offsets[:]))
        w1_q = quantise(w1_bf[:].rearrange("p t m j -> p (t m j)"), R, "w1")

        gout_raw = load_rows(gout, "gout_raw", "w1_raw")
        key_word_pool = load_words(keys_words, "key_word_pool", "w1_bf")

        zh = []
        mean_sq = sb.tile([P, CHUNKS, PAGES, PACK], F32, name="mean_sq")
        tab_pieces = []
        for first, count in ((0, 1), (1, 1), (2, 2)):
            words = sb.tile([P, count * CHUNK], U32, name="tab_words%d" % first, align_bytes=64)
            nc.vector.tensor_copy(
                words[:], tab_word_pool[:].bitcast(U32).indirect(offsets[:, PAGES * first : PAGES * (first + count)])
            )
            tab_pieces.extend(words[:, CHUNK * n : CHUNK * (n + 1)] for n in range(count))
        for c in range(CHUNKS):
            bank = ps.tile([P, PACK, CHUNK], F32, name="zh%d" % c)
            for t in range(PACK):
                nc.tensor.matmul_mx(
                    out=bank[:, t, :],
                    lhsT=w1_q[0][:, P * t : P * (t + 1)].bitcast(FP8X4),
                    lhsT_scale=w1_q[1][:, P * t : P * (t + 1)],
                    rhs=tab_pieces[c].bitcast(FP8X4),
                    rhs_scale=tab_scale[:, CHUNK * c : CHUNK * (c + 1)],
                    start=True,
                    stop=True,
                )
            zh.append(bank)

        def interleave(raw, name, tag):
            bf = sb.tile([P, Q, PACK], BF16, name=name, tag=tag, align_bytes=64)
            nc.scalar.copy(
                bf[:].rearrange("p (c i) j -> p c j i", i=4), raw.rearrange("p j (c i) -> p c j i", i=4)
            )
            return bf[:].rearrange("p c j -> p (c j)")

        query_bf = interleave(query_raw[:], "query_bf", "query_bf")
        gain_sb = load_feature_vector(gain, "gain_sb", "query_raw")
        key_scale = sb.tile([P, I], U8, name="key_scale", tag="tab_word_pool", align_bytes=64)
        nc.vector.tensor_copy(key_scale[:], key_scale_pool[:].indirect(offsets[:]))
        query_q = quantise(query_bf, Q, "query")
        hsc_sb = load_feature_vector(hsc, "hsc_sb", "query_bf")

        for c in range(CHUNKS):
            sq = sb.tile([P, PACK, CHUNK], F32, name="sq%d" % c, tag="sq%d" % c, align_bytes=64)
            nc.scalar.activation(sq[:], zh[c][:], ACT.Square)
            nc.vector.tensor_reduce(
                mean_sq[:, c], sq[:].rearrange("p t (g j) -> p g t j", j=PAGE), AXIS_X, ALU.add
            )

        gout_bf = interleave(gout_raw[:], "gout_bf", "w1_codes")

        inv_rms = sb.tile([P, CHUNKS * PAGES, PACK], F32, name="inv_rms")
        nc.scalar.activation(
            inv_rms[:], mean_sq[:].rearrange("p c g t -> p (c g) t"), ACT.Abs_reciprocal_sqrt, bias=0.1, scale=1.0 / PAGE
        )

        key_words = sb.tile([P, I], U32, name="key_words", tag="sq%d" % (CHUNKS - 1), align_bytes=64)
        nc.vector.tensor_copy(key_words[:], key_word_pool[:].bitcast(U32).indirect(offsets[:]))
        scores = ps.tile([P, I], F32, name="scores")
        product(scores[:], query_q, slice(0, Q), (key_words, key_scale), slice(0, I))
        old_sb = sb.tile([P, T], F32, name="old_sb", tag="tab_word_pool", align_bytes=64)
        nc.sync.dma_start(old_sb[:], old)

        factor = sb.tile([P, CHUNKS * PAGES, PACK], F32, name="factor")
        nc.gpsimd.tensor_tensor(
            factor[:], inv_rms[:], gain_sb[:].unsqueeze(1).to_broadcast([P, G, PACK]), ALU.mult
        )

        gout_q = quantise(gout_bf, Q, "gout")

        activated = []
        for c in range(CHUNKS):
            pre = sb.tile([P, PAGES, PAGE, PACK], F32, name="pre%d" % c, tag="pre%d" % c)
            nc.vector.tensor_tensor(
                pre[:],
                zh[c][:].rearrange("p t (g j) -> p g j t", j=PAGE),
                factor[:, PAGES * c : PAGES * (c + 1), :].unsqueeze(2).to_broadcast([P, PAGES, PAGE, PACK]),
                ALU.mult,
            )
            hv = sb.tile([P, CHUNK, PACK], F32, name="hv%d" % c)
            nc.scalar.activation(
                hv[:].rearrange("p i t -> p (i t)"), pre[:].rearrange("p g j t -> p (g j t)"), ACT.Silu
            )
            activated.append(hv)

        neg_max = sb.tile([P, 1], F32, name="neg_max")
        nc.vector.tensor_reduce(neg_max[:], scores[:], AXIS_X, ALU.max, negate=True)

        c0 = ps.tile([P, I], F32, name="c0")
        hs1 = sb.tile([P, I, PACK], BF16, name="hs1", align_bytes=64)

        def scale_chunk(engine, c):
            engine.tensor_tensor(
                hs1[:, CHUNK * c : CHUNK * (c + 1), :],
                activated[c][:],
                hsc_sb[:].unsqueeze(1).to_broadcast([P, CHUNK, PACK]),
                ALU.mult,
            )

        def read_gradient(first, count):
            slots = slice(CHUNK * first, CHUNK * (first + count))
            hs1_q = quantise(hs1[:, slots, :].rearrange("p i t -> p (i t)"), count * CHUNK, "hs1q%d" % first)
            product(c0[:, slots], gout_q, slice(0, Q), hs1_q, slice(0, count * CHUNK))

        scale_chunk(nc.gpsimd, 0)
        scale_chunk(nc.vector, 1)
        scale_chunk(nc.vector, 2)
        read_gradient(0, 2)
        scale_chunk(nc.vector, 3)
        read_gradient(2, 1)
        read_gradient(3, 1)

        p_exp = sb.tile([P, I], F32, name="p_exp", tag="pre%d" % (CHUNKS - 1))
        z = sb.tile([P, 1], F32, name="z")
        nc.scalar.activation(p_exp[:], scores[:], ACT.Exp, bias=neg_max[:], accum_out=z[:])
        scaled_z = sb.tile([P, 2], F32, name="scaled_z")
        nc.scalar.activation(scaled_z[:], constants[:], ACT.Copy, scale=z[:])
        row_factors = sb.tile([P, 2], F32, name="row_factors")
        nc.vector.reciprocal(row_factors[:], scaled_z[:])

        direct = sb.tile([P, I], F32, name="direct")
        row_sum = sb.tile([P, 1], F32, name="row_sum")
        nc.vector.scalar_tensor_tensor(
            direct[:], c0[:], row_factors[:, 0:1], p_exp[:], ALU.mult, ALU.mult, accum_out=row_sum[:]
        )
        through_z = sb.tile([P, I], F32, name="through_z")
        nc.vector.tensor_scalar(through_z[:], p_exp[:], row_sum[:], row_factors[:, 1:2], ALU.mult, ALU.mult)
        nc.vector.tensor_tensor(placed[:].indirect(offsets[:]), direct[:], through_z[:], ALU.add)

        start = 0
        for c, width in enumerate(OUT_WIDTHS):
            cols = slice(start, start + width)
            result = sb.tile([P, width], F32, name="result%d" % c)
            nc.vector.tensor_tensor(result[:], placed[:, cols], old_sb[:, cols], ALU.add)
            (nc.sync if c % 2 == 0 else nc.scalar).dma_start(out[:, cols], result[:])
            start = start + width
